import numpy as np
import ml_dtypes


def mxq(x, axis, fmt="e4m3"):
    dtype, down = {"e4m3": (ml_dtypes.float8_e4m3fn, 7), "e5m2": (ml_dtypes.float8_e5m2, 14)}[fmt]
    v = np.moveaxis(np.asarray(x, np.float32).astype(ml_dtypes.bfloat16).astype(np.float64), axis, -1)
    blocks = v.reshape(v.shape[:-1] + (-1, 32))
    amax = np.abs(blocks).max(-1, keepdims=True)
    byte = np.maximum(np.where(amax > 0, np.frexp(amax)[1] - 1 + 127, 0) - down, 1)
    scale = np.exp2(byte - 127.0)
    codes = (blocks / scale).astype(np.float32).astype(dtype).astype(np.float64)
    return np.moveaxis((codes * scale).reshape(v.shape), -1, axis)


WIDE = False


def mx_kscale(k):
    if not WIDE:
        return np.ones(k)
    levels = np.array([10, -10, 5, -5, 0])
    if k % 512:
        return np.exp2(np.random.permutation(np.resize(levels, k // 32))).repeat(32)
    a = np.empty((k // 512, 16))
    for p in range(k // 512):
        a[p, :8] = np.random.permutation(np.resize(levels, 8))
        for g in range(8):
            far = levels[np.abs(levels - a[p, g]) >= 10]
            a[p, g + 8] = far[np.random.randint(len(far))]
    return np.exp2(a.ravel()).repeat(32)


def f64(x):
    return np.asarray(x).astype(np.float64)


def striped(idx):
    return np.tile(np.asarray(idx).reshape(-1, 16).T, (8, 1)).astype(np.uint16)


def unstriped(offs):
    return offs[:16].T.reshape(-1).astype(np.int64)


B, N, T, D, DV, NQ = 2, 512, 2048, 512, 512, 128
PAGE = 64


def setup_inputs():
    n = np.random.standard_normal
    pages = np.random.permutation(T // PAGE)[:B * N // PAGE]
    idx = (pages[:, None] * PAGE + np.arange(PAGE)[None, :]).reshape(-1)
    s = mx_kscale(D)[:, None]
    u = np.ones(T)
    u[idx] = mx_kscale(B * N)
    r = np.random.uniform(0.5, 2.0, T)
    raw = n((D, T)) / s / (u * r)
    return {
        "qT": (n((B, D, NQ)) * s * (1.00 / np.sqrt(D))).astype(np.float32),
        "cT": raw.astype(np.float32),
        "ts": np.tile(u * r, (128, 1)).astype(np.float32),
        "sink": (2.0 + 3.0 * n((B, NQ, 1))).astype(np.float32),
        "ch": np.tile(s[:, 0] * np.random.uniform(0.5, 2.0, D), (128, 1)).astype(np.float32),
        "offs": striped(idx),
    }


def reference(qT, cT, ts, sink, ch, offs):
    idx = unstriped(offs)
    c = f64(cT)
    pick = lambda x: x[:, idx].reshape(x.shape[0], B, N).transpose(1, 0, 2)
    q = f64(qT)
    score = mxq(q, 1, "e4m3").transpose(0, 2, 1) @ mxq(pick(c), 1, "e4m3")
    score = score * pick(f64(ts))[:, :1, :]
    m = np.maximum(score.max(-1, keepdims=True), f64(sink))
    p = np.exp(score - m)
    total = p.sum(-1, keepdims=True) + np.exp(f64(sink) - m)
    w = p * pick(f64(ts))[:, :1, :]
    y = mxq(w, 2, "e4m3") @ mxq(pick(c).transpose(0, 2, 1), 1, "e4m3")
    y = y / total
    y = y * f64(ch)[:1]
    return y

@@ -1,0 +1,196 @@
+from contextlib import ExitStack
+
+import concourse.mybir as mybir
+from concourse.masks import make_identity
+
+B, N, T, D, NQ = 2, 512, 2048, 512, 128
+P = 128
+FLOPS = 4 * B * N * D * NQ
+
+F32 = mybir.dt.float32
+BF16 = mybir.dt.bfloat16
+U32 = mybir.dt.uint32
+U16 = mybir.dt.uint16
+U8 = mybir.dt.uint8
+FP8X4 = mybir.dt.float8_e4m3fn_x4
+MULT = mybir.AluOpType.mult
+MIN = mybir.AluOpType.min
+EXP = mybir.ActivationFunctionType.Exp
+AX = mybir.AxisListType.X
+
+
+def tile_attend_x_mla_sink_kernel(tc, qT, cT, ts, sink, ch, offs, out):
+    nc = tc.nc
+    with ExitStack() as ctx:
+        lists = ctx.enter_context(tc.tile_pool(name="lists", bufs=1))
+        keep = ctx.enter_context(tc.tile_pool(name="keep", bufs=1))
+        psum = ctx.enter_context(tc.psum_pool(name="psum", bufs=1))
+
+        def sb(shape, dtype, name):
+            return keep.tile(shape, dtype, name=name, align_bytes=64)
+
+        offsets = lists.tile([P, B * N // 16], U16, name="offsets")
+        nc.sync.dma_start(offsets[:], offs)
+
+        sink_sb = sb([P, B], F32, "sink_sb")
+        nc.scalar.dma_start(out=sink_sb[:], in_=sink.rearrange("b q o -> q (b o)"))
+        tsx = sb([P, P], F32, "tsx")
+        nc.gpsimd.memset(tsx[:], 0.0)
+        nc.scalar.dma_start(out=tsx[0:16, :], in_=ts[0:1, :].rearrange("o (j c) -> (o j) c", c=P))
+        ident = sb([P, P], F32, "ident")
+        make_identity(nc, ident[:])
+
+        cv = cT.rearrange("(p t) c -> p t c", t=4)
+        planes = []
+        for t in range(4):
+            pl = sb([P, T], F32, f"plane{t}")
+            nc.sync.dma_start(out=pl[:], in_=cv[:, t, :])
+            planes.append(pl)
+        qraw = sb([P, B, 4, NQ], F32, "qraw")
+        nc.sync.dma_start(out=qraw[:], in_=qT.rearrange("b (p t) q -> p b t q", t=4))
+        ch_sb = sb([P, D], F32, "ch_sb")
+        nc.sync.dma_start(out=ch_sb[:], in_=ch)
+
+        warm = sb([P, 1], F32, "warm")
+        nc.vector.memset(warm[:], 0.0)
+        nc.scalar.activation(out=warm[:], in_=warm[:], func=EXP)
+
+        xps = psum.tile([P, 512], F32, name="xps", tag="x", bufs=4)
+        nc.tensor.transpose(xps[:, 0:P], tsx[:], ident[:])
+        tsc = sb([P, 16], F32, "tsc")
+        nc.vector.tensor_copy(out=tsc[:], in_=xps[:, 0:16])
+        tsw = sb([P, T], F32, "tsw")
+        for c in range(4):
+            bps = psum.tile([P, 512], F32, name="bps", tag="x", bufs=4)
+            for j in range(4):
+                jj = 4 * c + j
+                nc.tensor.transpose(bps[:, j * P:(j + 1) * P], tsc[:, jj:jj + 1].to_broadcast([P, P]), ident[:])
+            if c % 2 == 0:
+                nc.scalar.copy(out=tsw[:, c * 512:(c + 1) * 512], in_=bps[:])
+            else:
+                nc.vector.tensor_copy(out=tsw[:, c * 512:(c + 1) * 512], in_=bps[:])
+
+        na, nm, l, rl = [], [], [], []
+        for b in range(B):
+            a_t = sb([P, 516], F32, f"na{b}")
+            nc.vector.memset(a_t[:, 512:516], 2.0 ** 126)
+            nc.vector.tensor_scalar(out=a_t[:, 512:513], in0=sink_sb[:, b:b + 1], scalar1=-1.0, scalar2=None, op0=MULT)
+            na.append(a_t)
+            nm.append(sb([P, 1], F32, f"nm{b}"))
+            l.append(sb([P, 1], F32, f"l{b}"))
+            rl.append(sb([P, 1], F32, f"rl{b}"))
+
+        g = [[sb([P, 2, N], F32, f"g{pr}_{b}") for b in range(B)] for pr in range(2)]
+        ki = [sb([P, N, 2, 2], BF16, f"ki{b}") for b in range(B)]
+        vt = [sb([P, D, 4], BF16, f"vt{b}") for b in range(B)]
+        vq = [sb([P, D], U32, f"vq{b}") for b in range(B)]
+        vs = [sb([P, D], U8, f"vs{b}") for b in range(B)]
+        tsg = [sb([P, N], F32, f"tsg{b}") for b in range(B)]
+        ts4 = [sb([P, 4], F32, f"ts4_{b}") for b in range(B)]
+
+        def offs_of(b):
+            return offsets[:, b * 32:(b + 1) * 32]
+
+        def gather(t, b):
+            nc.vector.tensor_copy(g[t // 2][b][:, t % 2, :], planes[t][:].indirect(offs_of(b)))
+
+        def values(t, b):
+            vb = sb([P, N], BF16, f"vb{t}_{b}")
+            nc.scalar.copy(out=vb[:], in_=g[t // 2][b][:, t % 2, :])
+            words = vb[:].bitcast(F32)
+            vps = psum.tile([P, 512], F32, name="vps", tag="x", bufs=4)
+            for u in range(2):
+                nc.tensor.transpose(vps[:, u * P:(u + 1) * P], words[:, u:N // 2:2], ident[:])
+            nc.scalar.copy(
+                out=vt[b][:, t * P:(t + 1) * P, :].rearrange("m d s -> m (d s)").bitcast(F32).rearrange("m (d u) -> m d u", u=2),
+                in_=vps[:, 0:2 * P].rearrange("m (u d) -> m d u", u=2),
+            )
+
+        def quant_values(t, b):
+            cols = slice(t * P, (t + 1) * P)
+            nc.vector.quantize_mx(
+                out=vq[b][:, cols].bitcast(FP8X4), scales=vs[b][:, cols],
+                in_=vt[b][:, cols, :].rearrange("m d s -> m (d s)"))
+
+        def pair(pr, b):
+            nc.vector.tensor_copy(
+                out=ki[b][:, :, pr, :].rearrange("p (c i) j -> p c j i", i=4),
+                in_=g[pr][b][:].rearrange("p j (c i) -> p c j i", i=4))
+
+        for t in range(3):
+            for b in range(B):
+                gather(t, b)
+            for b in range(B):
+                values(t, b)
+            for b in range(B):
+                quant_values(t, b)
+            if t == 1:
+                for b in range(B):
+                    pair(0, b)
+                for b in range(B):
+                    nc.vector.tensor_copy(tsg[b][:], tsw[:].indirect(offs_of(b)))
+                    tps = psum.tile([P, 512], F32, name="tps", tag="x", bufs=4)
+                    for s in range(4):
+                        nc.tensor.transpose(tps[:, s * P:(s + 1) * P], tsg[b][:, s:N:4], ident[:])
+                    nc.vector.tensor_copy(out=ts4[b][:], in_=tps[:, 0:512:P])
+
+        gather(3, 0)
+        gather(3, 1)
+        pair(1, 0)
+        qi = sb([P, B, NQ, 4], BF16, "qi")
+        for b in range(B):
+            nc.scalar.copy(out=qi[:, b].rearrange("p (c i) t -> p c t i", i=4),
+                           in_=qraw[:, b].rearrange("p t (c i) -> p c t i", i=4))
+        qq = sb([P, B * NQ], U32, "qq")
+        qs = sb([P, B * NQ], U8, "qs")
+        nc.vector.quantize_mx(out=qq[:].bitcast(FP8X4), scales=qs[:], in_=qi[:].rearrange("p b q t -> p (b q t)"))
+
+        def scores(b):
+            kq = sb([P, N], U32, f"kq{b}")
+            ks = sb([P, N], U8, f"ks{b}")
+            nc.vector.quantize_mx(out=kq[:].bitcast(FP8X4), scales=ks[:], in_=ki[b][:].rearrange("p s a j -> p (s a j)"))
+            sps = psum.tile([P, N], F32, name=f"sps{b}")
+            qc = slice(b * NQ, (b + 1) * NQ)
+            nc.tensor.matmul_mx(sps[:], lhsT=qq[:, qc].bitcast(FP8X4), lhsT_scale=qs[:, qc],
+                                rhs=kq[:].bitcast(FP8X4), rhs_scale=ks[:], start=True, stop=True)
+            return sps
+
+        def softmax(b, sps):
+            nc.vector.scalar_tensor_tensor(out=na[b][:, 0:N], in0=sps[:], scalar=-1.0, in1=tsg[b][:], op0=MULT, op1=MULT)
+            nc.vector.tensor_reduce(out=nm[b][:], in_=na[b][:, 0:N + 1], axis=AX, op=MIN)
+            p = sb([P, 4, 129], F32, f"p{b}")
+            nc.scalar.activation(out=p[:].rearrange("q s m -> q m s"), in_=na[b][:].rearrange("q (m s) -> q m s", s=4),
+                                 func=EXP, bias=nm[b][:], scale=-1.0, accum_out=l[b][:])
+            pps = psum.tile([P, 4, P], F32, name="pps", tag="x", bufs=4)
+            for s in range(4):
+                nc.tensor.transpose(pps[:, s, :], p[:, s, 0:P], ident[:])
+            wi = sb([P, NQ, 4], BF16, f"wi{b}")
+            nc.vector.tensor_tensor(out=wi[:], in0=pps[:].rearrange("m s q -> m q s"),
+                                    in1=ts4[b][:].unsqueeze(1).to_broadcast([P, NQ, 4]), op=MULT)
+            wq = sb([P, NQ], U32, f"wq{b}")
+            ws = sb([P, NQ], U8, f"ws{b}")
+            nc.vector.quantize_mx(out=wq[:].bitcast(FP8X4), scales=ws[:], in_=wi[:].rearrange("m q s -> m (q s)"))
+            nc.vector.reciprocal(out=rl[b][:], in_=l[b][:])
+            return wq, ws
+
+        def finish(b, wq, ws):
+            yps = psum.tile([P, D], F32, name=f"yps{b}")
+            nc.tensor.matmul_mx(yps[:], lhsT=wq[:].bitcast(FP8X4), lhsT_scale=ws[:],
+                                rhs=vq[b][:].bitcast(FP8X4), rhs_scale=vs[b][:], start=True, stop=True)
+            o = sb([P, D], F32, f"o{b}")
+            nc.vector.scalar_tensor_tensor(
+                out=o[:].rearrange("q (p t) -> q p t", t=4), in0=yps[:].rearrange("q (t p) -> q p t", t=4),
+                scalar=rl[b][:], in1=ch_sb[:].rearrange("q (p t) -> q p t", t=4), op0=MULT, op1=MULT)
+            nc.sync.dma_start(out=out[b], in_=o[:])
+
+        s0 = scores(0)
+        w0 = softmax(0, s0)
+        values(3, 0)
+        pair(1, 1)
+        s1 = scores(1)
+        quant_values(3, 0)
+        w1 = softmax(1, s1)
+        finish(0, w0[0], w0[1])
+        values(3, 1)
+        quant_values(3, 1)
+        finish(1, w1[0], w1[1])

@@ -14,6 +14,7 @@ U16 = mybir.dt.uint16
 U8 = mybir.dt.uint8
 FP8X4 = mybir.dt.float8_e4m3fn_x4
 MULT = mybir.AluOpType.mult
+ADD = mybir.AluOpType.add
 MIN = mybir.AluOpType.min
 EXP = mybir.ActivationFunctionType.Exp
 AX = mybir.AxisListType.X
@@ -29,126 +30,109 @@ def tile_attend_x_mla_sink_kernel(tc, qT, cT, ts, sink, ch, offs, out):
         def sb(shape, dtype, name):
             return keep.tile(shape, dtype, name=name, align_bytes=64)
 
+        def bank(name, shape=(P, 512)):
+            return psum.tile(list(shape), F32, name=name, tag="x", bufs=4)
+
+        tsx = sb([P, P], F32, "tsx")
+        nc.vector.memset(tsx[:], 0.0)
+        nc.sync.dma_start(out=tsx[0:16, :], in_=ts[0:1, :].rearrange("o (j c) -> (o j) c", c=P))
         offsets = lists.tile([P, B * N // 16], U16, name="offsets")
         nc.sync.dma_start(offsets[:], offs)
 
-        sink_sb = sb([P, B], F32, "sink_sb")
-        nc.scalar.dma_start(out=sink_sb[:], in_=sink.rearrange("b q o -> q (b o)"))
-        tsx = sb([P, P], F32, "tsx")
-        nc.gpsimd.memset(tsx[:], 0.0)
-        nc.scalar.dma_start(out=tsx[0:16, :], in_=ts[0:1, :].rearrange("o (j c) -> (o j) c", c=P))
         ident = sb([P, P], F32, "ident")
         make_identity(nc, ident[:])
+        sink_sb = sb([P, B], F32, "sink_sb")
+        nc.scalar.dma_start(out=sink_sb[:], in_=sink.rearrange("b q o -> q (b o)"))
 
         cv = cT.rearrange("(p t) c -> p t c", t=4)
-        planes = []
-        for t in range(4):
-            pl = sb([P, T], F32, f"plane{t}")
+        planes = {}
+
+        def load_plane(t):
+            pl = keep.tile([P, T], F32, name=f"plane{t}", tag=f"r{t}", bufs=1, align_bytes=64)
             nc.sync.dma_start(out=pl[:], in_=cv[:, t, :])
-            planes.append(pl)
-        qraw = sb([P, B, 4, NQ], F32, "qraw")
-        nc.sync.dma_start(out=qraw[:], in_=qT.rearrange("b (p t) q -> p b t q", t=4))
-        ch_sb = sb([P, D], F32, "ch_sb")
-        nc.sync.dma_start(out=ch_sb[:], in_=ch)
+            planes[t] = pl
+
+        for t in range(4):
+            load_plane(t)
+
 
         warm = sb([P, 1], F32, "warm")
-        nc.vector.memset(warm[:], 0.0)
+        nc.gpsimd.memset(warm[:], 0.0)
         nc.scalar.activation(out=warm[:], in_=warm[:], func=EXP)
-
-        xps = psum.tile([P, 512], F32, name="xps", tag="x", bufs=4)
-        nc.tensor.transpose(xps[:, 0:P], tsx[:], ident[:])
-        tsc = sb([P, 16], F32, "tsc")
-        nc.vector.tensor_copy(out=tsc[:], in_=xps[:, 0:16])
-        tsw = sb([P, T], F32, "tsw")
-        for c in range(4):
-            bps = psum.tile([P, 512], F32, name="bps", tag="x", bufs=4)
-            for j in range(4):
-                jj = 4 * c + j
-                nc.tensor.transpose(bps[:, j * P:(j + 1) * P], tsc[:, jj:jj + 1].to_broadcast([P, P]), ident[:])
-            if c % 2 == 0:
-                nc.scalar.copy(out=tsw[:, c * 512:(c + 1) * 512], in_=bps[:])
-            else:
-                nc.vector.tensor_copy(out=tsw[:, c * 512:(c + 1) * 512], in_=bps[:])
 
         na, nm, l, rl = [], [], [], []
         for b in range(B):
             a_t = sb([P, 516], F32, f"na{b}")
-            nc.vector.memset(a_t[:, 512:516], 2.0 ** 126)
-            nc.vector.tensor_scalar(out=a_t[:, 512:513], in0=sink_sb[:, b:b + 1], scalar1=-1.0, scalar2=None, op0=MULT)
+            nc.gpsimd.memset(a_t[:, 512:516], 2.0 ** 126)
+            nc.gpsimd.tensor_scalar(out=a_t[:, 512:513], in0=sink_sb[:, b:b + 1], scalar1=-1.0, scalar2=0.0, op0=MULT, op1=ADD)
             na.append(a_t)
             nm.append(sb([P, 1], F32, f"nm{b}"))
             l.append(sb([P, 1], F32, f"l{b}"))
             rl.append(sb([P, 1], F32, f"rl{b}"))
 
-        g = [[sb([P, 2, N], F32, f"g{pr}_{b}") for b in range(B)] for pr in range(2)]
-        ki = [sb([P, N, 2, 2], BF16, f"ki{b}") for b in range(B)]
-        vt = [sb([P, D, 4], BF16, f"vt{b}") for b in range(B)]
+        kw = sb([P, B * N, 2], U32, "kw")
+        kb = kw[:].rearrange("p s w -> p (s w)").bitcast(BF16).rearrange("p (s t) -> p s t", t=4)
+        kf = kw[:].rearrange("p s w -> p (s w)").bitcast(F32).rearrange("p (s w) -> p s w", w=2)
+        vt = [sb([P, 2, 2, P, 4], BF16, f"vt{b}") for b in range(B)]
         vq = [sb([P, D], U32, f"vq{b}") for b in range(B)]
         vs = [sb([P, D], U8, f"vs{b}") for b in range(B)]
-        tsg = [sb([P, N], F32, f"tsg{b}") for b in range(B)]
+        tsg = sb([P, B * N], F32, "tsg")
         ts4 = [sb([P, 4], F32, f"ts4_{b}") for b in range(B)]
 
-        def offs_of(b):
-            return offsets[:, b * 32:(b + 1) * 32]
+        def slots(b):
+            return slice(b * N, (b + 1) * N)
 
-        def gather(t, b):
-            nc.vector.tensor_copy(g[t // 2][b][:, t % 2, :], planes[t][:].indirect(offs_of(b)))
+        tsw = sb([P, T], F32, "tsw")
 
-        def values(t, b):
-            vb = sb([P, N], BF16, f"vb{t}_{b}")
-            nc.scalar.copy(out=vb[:], in_=g[t // 2][b][:, t % 2, :])
-            words = vb[:].bitcast(F32)
-            vps = psum.tile([P, 512], F32, name="vps", tag="x", bufs=4)
-            for u in range(2):
-                nc.tensor.transpose(vps[:, u * P:(u + 1) * P], words[:, u:N // 2:2], ident[:])
-            nc.scalar.copy(
-                out=vt[b][:, t * P:(t + 1) * P, :].rearrange("m d s -> m (d s)").bitcast(F32).rearrange("m (d u) -> m d u", u=2),
-                in_=vps[:, 0:2 * P].rearrange("m (u d) -> m d u", u=2),
-            )
+        def scales_road():
+            xps = bank("xps")
+            nc.tensor.transpose(xps[:, 0:P], tsx[:], ident[:])
+            tsc = sb([P, 16], F32, "tsc")
+            nc.scalar.copy(out=tsc[:], in_=xps[:, 0:16])
+            for c in range(4):
+                bps = bank("bps")
+                for j in range(4):
+                    jj = 4 * c + j
+                    nc.tensor.transpose(bps[:, j * P:(j + 1) * P], tsc[:, jj:jj + 1].to_broadcast([P, P]), ident[:])
+                nc.scalar.copy(out=tsw[:, c * 512:(c + 1) * 512], in_=bps[:])
 
-        def quant_values(t, b):
-            cols = slice(t * P, (t + 1) * P)
+        def scales_gather():
+            nc.vector.tensor_copy(tsg[:], tsw[:].indirect(offsets[:]))
+            for b in range(B):
+                tps = bank("tps")
+                for s in range(4):
+                    nc.tensor.transpose(tps[:, s * P:(s + 1) * P], tsg[:, b * N + s:(b + 1) * N:4], ident[:])
+                nc.scalar.copy(out=ts4[b][:], in_=tps[:, 0:512:P])
+
+        def values(u, b):
+            vps = bank("vps")
+            for s in range(4):
+                nc.tensor.transpose(vps[:, s * P:(s + 1) * P], kf[:, b * N + s:(b + 1) * N:4, u], ident[:])
+            for j in range(2):
+                nc.scalar.copy(out=vt[b][:, u, j],
+                               in_=vps[:].bitcast(BF16).rearrange("m (s p j) -> m j p s", s=4, j=2)[:, j])
+
+        def quant_values(u, b):
+            cols = slice(u * 2 * P, (u + 1) * 2 * P)
             nc.vector.quantize_mx(
                 out=vq[b][:, cols].bitcast(FP8X4), scales=vs[b][:, cols],
-                in_=vt[b][:, cols, :].rearrange("m d s -> m (d s)"))
+                in_=vt[b][:, u].rearrange("m j p s -> m (j p s)"))
 
-        def pair(pr, b):
-            nc.vector.tensor_copy(
-                out=ki[b][:, :, pr, :].rearrange("p (c i) j -> p c j i", i=4),
-                in_=g[pr][b][:].rearrange("p j (c i) -> p c j i", i=4))
-
-        for t in range(3):
-            for b in range(B):
-                gather(t, b)
-            for b in range(B):
-                values(t, b)
-            for b in range(B):
-                quant_values(t, b)
-            if t == 1:
-                for b in range(B):
-                    pair(0, b)
-                for b in range(B):
-                    nc.vector.tensor_copy(tsg[b][:], tsw[:].indirect(offs_of(b)))
-                    tps = psum.tile([P, 512], F32, name="tps", tag="x", bufs=4)
-                    for s in range(4):
-                        nc.tensor.transpose(tps[:, s * P:(s + 1) * P], tsg[b][:, s:N:4], ident[:])
-                    nc.vector.tensor_copy(out=ts4[b][:], in_=tps[:, 0:512:P])
-
-        gather(3, 0)
-        gather(3, 1)
-        pair(1, 0)
         qi = sb([P, B, NQ, 4], BF16, "qi")
-        for b in range(B):
-            nc.scalar.copy(out=qi[:, b].rearrange("p (c i) t -> p c t i", i=4),
-                           in_=qraw[:, b].rearrange("p t (c i) -> p c t i", i=4))
         qq = sb([P, B * NQ], U32, "qq")
         qs = sb([P, B * NQ], U8, "qs")
-        nc.vector.quantize_mx(out=qq[:].bitcast(FP8X4), scales=qs[:], in_=qi[:].rearrange("p b q t -> p (b q t)"))
+
+        def queries():
+            for b in range(B):
+                nc.scalar.copy(out=qi[:, b].rearrange("p (c i) t -> p c t i", i=4),
+                               in_=qraw[:, b].rearrange("p t (c i) -> p c t i", i=4))
+            nc.vector.quantize_mx(out=qq[:].bitcast(FP8X4), scales=qs[:], in_=qi[:].rearrange("p b q t -> p (b q t)"))
 
         def scores(b):
             kq = sb([P, N], U32, f"kq{b}")
             ks = sb([P, N], U8, f"ks{b}")
-            nc.vector.quantize_mx(out=kq[:].bitcast(FP8X4), scales=ks[:], in_=ki[b][:].rearrange("p s a j -> p (s a j)"))
+            nc.vector.quantize_mx(out=kq[:].bitcast(FP8X4), scales=ks[:],
+                                  in_=kb[:, slots(b), :].rearrange("p s t -> p (s t)"))
             sps = psum.tile([P, N], F32, name=f"sps{b}")
             qc = slice(b * NQ, (b + 1) * NQ)
             nc.tensor.matmul_mx(sps[:], lhsT=qq[:, qc].bitcast(FP8X4), lhsT_scale=qs[:, qc],
@@ -156,12 +140,12 @@ def tile_attend_x_mla_sink_kernel(tc, qT, cT, ts, sink, ch, offs, out):
             return sps
 
         def softmax(b, sps):
-            nc.vector.scalar_tensor_tensor(out=na[b][:, 0:N], in0=sps[:], scalar=-1.0, in1=tsg[b][:], op0=MULT, op1=MULT)
+            nc.vector.scalar_tensor_tensor(out=na[b][:, 0:N], in0=sps[:], scalar=-1.0, in1=tsg[:, slots(b)], op0=MULT, op1=MULT)
             nc.vector.tensor_reduce(out=nm[b][:], in_=na[b][:, 0:N + 1], axis=AX, op=MIN)
             p = sb([P, 4, 129], F32, f"p{b}")
             nc.scalar.activation(out=p[:].rearrange("q s m -> q m s"), in_=na[b][:].rearrange("q (m s) -> q m s", s=4),
                                  func=EXP, bias=nm[b][:], scale=-1.0, accum_out=l[b][:])
-            pps = psum.tile([P, 4, P], F32, name="pps", tag="x", bufs=4)
+            pps = bank("pps", (P, 4, P))
             for s in range(4):
                 nc.tensor.transpose(pps[:, s, :], p[:, s, 0:P], ident[:])
             wi = sb([P, NQ, 4], BF16, f"wi{b}")
@@ -170,10 +154,10 @@ def tile_attend_x_mla_sink_kernel(tc, qT, cT, ts, sink, ch, offs, out):
             wq = sb([P, NQ], U32, f"wq{b}")
             ws = sb([P, NQ], U8, f"ws{b}")
             nc.vector.quantize_mx(out=wq[:].bitcast(FP8X4), scales=ws[:], in_=wi[:].rearrange("m q s -> m (q s)"))
-            nc.vector.reciprocal(out=rl[b][:], in_=l[b][:])
             return wq, ws
 
         def finish(b, wq, ws):
+            nc.vector.reciprocal(out=rl[b][:], in_=l[b][:])
             yps = psum.tile([P, D], F32, name=f"yps{b}")
             nc.tensor.matmul_mx(yps[:], lhsT=wq[:].bitcast(FP8X4), lhsT_scale=ws[:],
                                 rhs=vq[b][:].bitcast(FP8X4), rhs_scale=vs[b][:], start=True, stop=True)
@@ -183,14 +167,35 @@ def tile_attend_x_mla_sink_kernel(tc, qT, cT, ts, sink, ch, offs, out):
                 scalar=rl[b][:], in1=ch_sb[:].rearrange("q (p t) -> q p t", t=4), op0=MULT, op1=MULT)
             nc.sync.dma_start(out=out[b], in_=o[:])
 
+        def gather_plane(t, b=None):
+            if b is None:
+                nc.vector.tensor_copy(kb[:, :, t], planes[t][:].indirect(offsets[:]))
+            else:
+                nc.vector.tensor_copy(kb[:, slots(b), t], planes[t][:].indirect(offsets[:, b * 32:(b + 1) * 32]))
+
+        scales_road()
+        gather_plane(0)
+        qraw = keep.tile([P, B, 4, NQ], F32, name="qraw", tag="r0", bufs=1, align_bytes=64)
+        nc.sync.dma_start(out=qraw[:], in_=qT.rearrange("b (p t) q -> p b t q", t=4))
+        ch_sb = sb([P, D], F32, "ch_sb")
+        nc.sync.dma_start(out=ch_sb[:], in_=ch)
+        gather_plane(1)
+        values(0, 0)
+        values(0, 1)
+        scales_gather()
+        gather_plane(2)
+        gather_plane(3, 0)
+        queries()
         s0 = scores(0)
+        gather_plane(3, 1)
         w0 = softmax(0, s0)
-        values(3, 0)
-        pair(1, 1)
         s1 = scores(1)
-        quant_values(3, 0)
         w1 = softmax(1, s1)
+        values(1, 0)
+        quant_values(0, 0)
+        quant_values(1, 0)
         finish(0, w0[0], w0[1])
-        values(3, 1)
-        quant_values(3, 1)
+        values(1, 1)
+        quant_values(0, 1)
+        quant_values(1, 1)
         finish(1, w1[0], w1[1])

@@ -45,16 +45,11 @@ def tile_attend_x_mla_sink_kernel(tc, qT, cT, ts, sink, ch, offs, out):
         nc.scalar.dma_start(out=sink_sb[:], in_=sink.rearrange("b q o -> q (b o)"))
 
         cv = cT.rearrange("(p t) c -> p t c", t=4)
-        planes = {}
-
-        def load_plane(t):
+        planes = []
+        for t in range(4):
             pl = keep.tile([P, T], F32, name=f"plane{t}", tag=f"r{t}", bufs=1, align_bytes=64)
             nc.sync.dma_start(out=pl[:], in_=cv[:, t, :])
-            planes[t] = pl
-
-        for t in range(4):
-            load_plane(t)
-
+            planes.append(pl)
 
         warm = sb([P, 1], F32, "warm")
         nc.gpsimd.memset(warm[:], 0.0)
@@ -70,19 +65,17 @@ def tile_attend_x_mla_sink_kernel(tc, qT, cT, ts, sink, ch, offs, out):
             l.append(sb([P, 1], F32, f"l{b}"))
             rl.append(sb([P, 1], F32, f"rl{b}"))
 
-        kw = sb([P, B * N, 2], U32, "kw")
-        kb = kw[:].rearrange("p s w -> p (s w)").bitcast(BF16).rearrange("p (s t) -> p s t", t=4)
-        kf = kw[:].rearrange("p s w -> p (s w)").bitcast(F32).rearrange("p (s w) -> p s w", w=2)
-        vt = [sb([P, 2, 2, P, 4], BF16, f"vt{b}") for b in range(B)]
+        g = sb([P, 4, B * N], F32, "g")
+        vt = [sb([P, D, 4], BF16, f"vt{b}") for b in range(B)]
+        vtw = [v[:].rearrange("m d s -> m (d s)").bitcast(F32).rearrange("m (d u) -> m d u", u=2) for v in vt]
         vq = [sb([P, D], U32, f"vq{b}") for b in range(B)]
         vs = [sb([P, D], U8, f"vs{b}") for b in range(B)]
+        tsw = sb([P, T], F32, "tsw")
         tsg = sb([P, B * N], F32, "tsg")
         ts4 = [sb([P, 4], F32, f"ts4_{b}") for b in range(B)]
 
         def slots(b):
             return slice(b * N, (b + 1) * N)
-
-        tsw = sb([P, T], F32, "tsw")
 
         def scales_road():
             xps = bank("xps")
@@ -104,43 +97,66 @@ def tile_attend_x_mla_sink_kernel(tc, qT, cT, ts, sink, ch, offs, out):
                     nc.tensor.transpose(tps[:, s * P:(s + 1) * P], tsg[:, b * N + s:(b + 1) * N:4], ident[:])
                 nc.scalar.copy(out=ts4[b][:], in_=tps[:, 0:512:P])
 
-        def values(u, b):
+        def gather(t, b=None):
+            if b is None:
+                nc.vector.tensor_copy(g[:, t, :], planes[t][:].indirect(offsets[:]))
+            else:
+                nc.vector.tensor_copy(g[:, t, slots(b)], planes[t][:].indirect(offsets[:, b * 32:(b + 1) * 32]))
+
+        def values(t, eng):
+            vb = sb([P, B * N], BF16, f"vb{t}")
+            if eng == "A":
+                nc.scalar.copy(out=vb[:], in_=g[:, t, :])
+            else:
+                nc.vector.tensor_copy(out=vb[:], in_=g[:, t, :])
+            words = vb[:].bitcast(F32)
             vps = bank("vps")
-            for s in range(4):
-                nc.tensor.transpose(vps[:, s * P:(s + 1) * P], kf[:, b * N + s:(b + 1) * N:4, u], ident[:])
-            for j in range(2):
-                nc.scalar.copy(out=vt[b][:, u, j],
-                               in_=vps[:].bitcast(BF16).rearrange("m (s p j) -> m j p s", s=4, j=2)[:, j])
+            for b in range(B):
+                for u in range(2):
+                    k = 2 * b + u
+                    nc.tensor.transpose(vps[:, k * P:(k + 1) * P], words[:, b * N // 2 + u:(b + 1) * N // 2:2], ident[:])
+            for b in range(B):
+                nc.scalar.copy(out=vtw[b][:, t * P:(t + 1) * P, :],
+                               in_=vps[:, b * 2 * P:(b + 1) * 2 * P].rearrange("m (u d) -> m d u", u=2))
 
         def quant_values(u, b):
             cols = slice(u * 2 * P, (u + 1) * 2 * P)
             nc.vector.quantize_mx(
                 out=vq[b][:, cols].bitcast(FP8X4), scales=vs[b][:, cols],
-                in_=vt[b][:, u].rearrange("m j p s -> m (j p s)"))
+                in_=vt[b][:, cols, :].rearrange("m d s -> m (d s)"))
 
         qi = sb([P, B, NQ, 4], BF16, "qi")
         qq = sb([P, B * NQ], U32, "qq")
         qs = sb([P, B * NQ], U8, "qs")
 
-        def queries():
-            for b in range(B):
-                nc.scalar.copy(out=qi[:, b].rearrange("p (c i) t -> p c t i", i=4),
-                               in_=qraw[:, b].rearrange("p t (c i) -> p c t i", i=4))
-            nc.vector.quantize_mx(out=qq[:].bitcast(FP8X4), scales=qs[:], in_=qi[:].rearrange("p b q t -> p (b q t)"))
-
-        def scores(b):
-            kq = sb([P, N], U32, f"kq{b}")
-            ks = sb([P, N], U8, f"ks{b}")
-            nc.vector.quantize_mx(out=kq[:].bitcast(FP8X4), scales=ks[:],
-                                  in_=kb[:, slots(b), :].rearrange("p s t -> p (s t)"))
-            sps = psum.tile([P, N], F32, name=f"sps{b}")
+        def queries(b):
             qc = slice(b * NQ, (b + 1) * NQ)
-            nc.tensor.matmul_mx(sps[:], lhsT=qq[:, qc].bitcast(FP8X4), lhsT_scale=qs[:, qc],
-                                rhs=kq[:].bitcast(FP8X4), rhs_scale=ks[:], start=True, stop=True)
-            return sps
+            nc.scalar.copy(out=qi[:, b], in_=qraw[:, b].rearrange("p t q -> p q t"))
+            nc.vector.quantize_mx(out=qq[:, qc].bitcast(FP8X4), scales=qs[:, qc], in_=qi[:, b].rearrange("p q t -> p (q t)"))
 
-        def softmax(b, sps):
-            nc.vector.scalar_tensor_tensor(out=na[b][:, 0:N], in0=sps[:], scalar=-1.0, in1=tsg[:, slots(b)], op0=MULT, op1=MULT)
+        ki = [[sb([P, N // 2, 4], BF16, f"ki{b}_{h}") for h in range(2)] for b in range(B)]
+        kq = [sb([P, N], U32, f"kq{b}") for b in range(B)]
+        ks = [sb([P, N], U8, f"ks{b}") for b in range(B)]
+        sps = [psum.tile([P, N], F32, name=f"sps{b}") for b in range(B)]
+
+        def keys(b, h, eng):
+            lo = b * N + h * N // 2
+            x = g[:, :, lo:lo + N // 2].rearrange("p t s -> p s t")
+            if eng == "A":
+                nc.scalar.copy(out=ki[b][h][:], in_=x)
+            else:
+                nc.vector.tensor_copy(out=ki[b][h][:], in_=x)
+
+        def scores(b, h):
+            hc = slice(h * N // 2, (h + 1) * N // 2)
+            nc.vector.quantize_mx(out=kq[b][:, hc].bitcast(FP8X4), scales=ks[b][:, hc],
+                                  in_=ki[b][h][:].rearrange("p s t -> p (s t)"))
+            qc = slice(b * NQ, (b + 1) * NQ)
+            nc.tensor.matmul_mx(sps[b][:, hc], lhsT=qq[:, qc].bitcast(FP8X4), lhsT_scale=qs[:, qc],
+                                rhs=kq[b][:, hc].bitcast(FP8X4), rhs_scale=ks[b][:, hc], start=True, stop=True)
+
+        def softmax(b):
+            nc.vector.scalar_tensor_tensor(out=na[b][:, 0:N], in0=sps[b][:], scalar=-1.0, in1=tsg[:, slots(b)], op0=MULT, op1=MULT)
             nc.vector.tensor_reduce(out=nm[b][:], in_=na[b][:, 0:N + 1], axis=AX, op=MIN)
             p = sb([P, 4, 129], F32, f"p{b}")
             nc.scalar.activation(out=p[:].rearrange("q s m -> q m s"), in_=na[b][:].rearrange("q (m s) -> q m s", s=4),
@@ -167,35 +183,37 @@ def tile_attend_x_mla_sink_kernel(tc, qT, cT, ts, sink, ch, offs, out):
                 scalar=rl[b][:], in1=ch_sb[:].rearrange("q (p t) -> q p t", t=4), op0=MULT, op1=MULT)
             nc.sync.dma_start(out=out[b], in_=o[:])
 
-        def gather_plane(t, b=None):
-            if b is None:
-                nc.vector.tensor_copy(kb[:, :, t], planes[t][:].indirect(offsets[:]))
-            else:
-                nc.vector.tensor_copy(kb[:, slots(b), t], planes[t][:].indirect(offsets[:, b * 32:(b + 1) * 32]))
-
         scales_road()
-        gather_plane(0)
+        gather(0)
         qraw = keep.tile([P, B, 4, NQ], F32, name="qraw", tag="r0", bufs=1, align_bytes=64)
-        nc.sync.dma_start(out=qraw[:], in_=qT.rearrange("b (p t) q -> p b t q", t=4))
+        for b in range(B):
+            nc.sync.dma_start(out=qraw[:, b], in_=qT[b].rearrange("(p t) q -> p t q", t=4))
         ch_sb = sb([P, D], F32, "ch_sb")
         nc.sync.dma_start(out=ch_sb[:], in_=ch)
-        gather_plane(1)
-        values(0, 0)
-        values(0, 1)
+        values(0, "D")
+        gather(1)
+        values(1, "D")
         scales_gather()
-        gather_plane(2)
-        gather_plane(3, 0)
-        queries()
-        s0 = scores(0)
-        gather_plane(3, 1)
-        w0 = softmax(0, s0)
-        s1 = scores(1)
-        w1 = softmax(1, s1)
-        values(1, 0)
+        gather(2)
+        values(2, "D")
+        gather(3, 0)
+        keys(0, 0, "D")
+        queries(0)
+        keys(0, 1, "A")
+        scores(0, 0)
+        scores(0, 1)
         quant_values(0, 0)
+        quant_values(0, 1)
+        w0 = softmax(0)
+        gather(3, 1)
+        keys(1, 0, "D")
+        queries(1)
+        keys(1, 1, "A")
+        scores(1, 0)
+        scores(1, 1)
+        w1 = softmax(1)
+        values(3, "A")
         quant_values(1, 0)
         finish(0, w0[0], w0[1])
-        values(1, 1)
-        quant_values(0, 1)
         quant_values(1, 1)
         finish(1, w1[0], w1[1])

@@ -5,6 +5,7 @@ from concourse.masks import make_identity
 
 B, N, T, D, NQ = 2, 512, 2048, 512, 128
 P = 128
+H = N // 2
 FLOPS = 4 * B * N * D * NQ
 
 F32 = mybir.dt.float32
@@ -30,15 +31,17 @@ def tile_attend_x_mla_sink_kernel(tc, qT, cT, ts, sink, ch, offs, out):
         def sb(shape, dtype, name):
             return keep.tile(shape, dtype, name=name, align_bytes=64)
 
-        def bank(name, shape=(P, 512)):
-            return psum.tile(list(shape), F32, name=name, tag="x", bufs=4)
+        def slot(shape, name, k):
+            return keep.tile(shape, F32, name=name, tag=f"r{k}", bufs=1, align_bytes=64)
 
-        tsx = sb([P, P], F32, "tsx")
-        nc.vector.memset(tsx[:], 0.0)
-        nc.sync.dma_start(out=tsx[0:16, :], in_=ts[0:1, :].rearrange("o (j c) -> (o j) c", c=P))
+        def bank(name):
+            return psum.tile([P, 512], F32, name=name, tag="x", bufs=4)
+
+        def half_bank(name, b, h):
+            return psum.tile([P, 512], F32, name=name, tag=f"s{b}{h}", bufs=1)
+
         offsets = lists.tile([P, B * N // 16], U16, name="offsets")
         nc.sync.dma_start(offsets[:], offs)
-
         ident = sb([P, P], F32, "ident")
         make_identity(nc, ident[:])
         sink_sb = sb([P, B], F32, "sink_sb")
@@ -47,7 +50,7 @@ def tile_attend_x_mla_sink_kernel(tc, qT, cT, ts, sink, ch, offs, out):
         cv = cT.rearrange("(p t) c -> p t c", t=4)
         planes = []
         for t in range(4):
-            pl = keep.tile([P, T], F32, name=f"plane{t}", tag=f"r{t}", bufs=1, align_bytes=64)
+            pl = slot([P, T], f"plane{t}", t)
             nc.sync.dma_start(out=pl[:], in_=cv[:, t, :])
             planes.append(pl)
 
@@ -55,165 +58,242 @@ def tile_attend_x_mla_sink_kernel(tc, qT, cT, ts, sink, ch, offs, out):
         nc.gpsimd.memset(warm[:], 0.0)
         nc.scalar.activation(out=warm[:], in_=warm[:], func=EXP)
 
-        na, nm, l, rl = [], [], [], []
+        na = [sb([P, 516], F32, f"na{b}") for b in range(B)]
         for b in range(B):
-            a_t = sb([P, 516], F32, f"na{b}")
-            nc.gpsimd.memset(a_t[:, 512:516], 2.0 ** 126)
-            nc.gpsimd.tensor_scalar(out=a_t[:, 512:513], in0=sink_sb[:, b:b + 1], scalar1=-1.0, scalar2=0.0, op0=MULT, op1=ADD)
-            na.append(a_t)
-            nm.append(sb([P, 1], F32, f"nm{b}"))
-            l.append(sb([P, 1], F32, f"l{b}"))
-            rl.append(sb([P, 1], F32, f"rl{b}"))
-
+            nc.gpsimd.memset(na[b][:, 512:516], 2.0 ** 126)
+            nc.gpsimd.tensor_scalar(out=na[b][:, 512:513], in0=sink_sb[:, b:b + 1], scalar1=-1.0, scalar2=0.0, op0=MULT, op1=ADD)
+        nm = [sb([P, 1], F32, f"nm{b}") for b in range(B)]
+        l2 = [sb([P, 2], F32, f"l2_{b}") for b in range(B)]
+        rl = [sb([P, 1], F32, f"rl{b}") for b in range(B)]
         g = sb([P, 4, B * N], F32, "g")
-        vt = [sb([P, D, 4], BF16, f"vt{b}") for b in range(B)]
-        vtw = [v[:].rearrange("m d s -> m (d s)").bitcast(F32).rearrange("m (d u) -> m d u", u=2) for v in vt]
+        vb = [sb([P, B * N], BF16, f"vb{t}") for t in range(4)]
+        vt = [sb([P, 2, 4, 64, 4], BF16, f"vt{b}") for b in range(B)]
+        vtw = [v[:].rearrange("m h t p s -> m (h t p s)").bitcast(F32).rearrange("m (h t p u) -> m h t p u", h=2, t=4, u=2) for v in vt]
         vq = [sb([P, D], U32, f"vq{b}") for b in range(B)]
         vs = [sb([P, D], U8, f"vs{b}") for b in range(B)]
-        tsw = sb([P, T], F32, "tsw")
         tsg = sb([P, B * N], F32, "tsg")
         ts4 = [sb([P, 4], F32, f"ts4_{b}") for b in range(B)]
+        qi = [sb([P, NQ, 4], BF16, f"qi{b}") for b in range(B)]
+        qq = [sb([P, NQ], U32, f"qq{b}") for b in range(B)]
+        qs = [sb([P, NQ], U8, f"qs{b}") for b in range(B)]
+        ki = [[sb([P, H, 4], BF16, f"ki{b}_{h}") for h in range(2)] for b in range(B)]
+        kq = [sb([P, N], U32, f"kq{b}") for b in range(B)]
+        ks = [sb([P, N], U8, f"ks{b}") for b in range(B)]
+        p = [sb([P, 4, 129], F32, f"p{b}") for b in range(B)]
+        wi = [sb([P, NQ, 4], BF16, f"wi{b}") for b in range(B)]
+        wq = [sb([P, NQ], U32, f"wq{b}") for b in range(B)]
+        ws = [sb([P, NQ], U8, f"ws{b}") for b in range(B)]
+        o = [sb([P, D], F32, f"o{b}") for b in range(B)]
+        qraw = [None, None]
+        tile = {}
 
-        def slots(b):
-            return slice(b * N, (b + 1) * N)
-
-        def scales_road():
-            xps = bank("xps")
-            nc.tensor.transpose(xps[:, 0:P], tsx[:], ident[:])
-            tsc = sb([P, 16], F32, "tsc")
-            nc.scalar.copy(out=tsc[:], in_=xps[:, 0:16])
-            for c in range(4):
-                bps = bank("bps")
-                for j in range(4):
-                    jj = 4 * c + j
-                    nc.tensor.transpose(bps[:, j * P:(j + 1) * P], tsc[:, jj:jj + 1].to_broadcast([P, P]), ident[:])
-                nc.scalar.copy(out=tsw[:, c * 512:(c + 1) * 512], in_=bps[:])
-
-        def scales_gather():
-            nc.vector.tensor_copy(tsg[:], tsw[:].indirect(offsets[:]))
-            for b in range(B):
-                tps = bank("tps")
-                for s in range(4):
-                    nc.tensor.transpose(tps[:, s * P:(s + 1) * P], tsg[:, b * N + s:(b + 1) * N:4], ident[:])
-                nc.scalar.copy(out=ts4[b][:], in_=tps[:, 0:512:P])
-
-        def gather(t, b=None):
-            if b is None:
-                nc.vector.tensor_copy(g[:, t, :], planes[t][:].indirect(offsets[:]))
-            else:
-                nc.vector.tensor_copy(g[:, t, slots(b)], planes[t][:].indirect(offsets[:, b * 32:(b + 1) * 32]))
-
-        def values(t, eng):
-            vb = sb([P, B * N], BF16, f"vb{t}")
+        def copy(eng, out, in_):
             if eng == "A":
-                nc.scalar.copy(out=vb[:], in_=g[:, t, :])
+                nc.scalar.copy(out=out, in_=in_)
+            elif eng == "D":
+                nc.vector.tensor_copy(out=out, in_=in_)
             else:
-                nc.vector.tensor_copy(out=vb[:], in_=g[:, t, :])
-            words = vb[:].bitcast(F32)
-            vps = bank("vps")
+                nc.gpsimd.tensor_scalar(out=out, in0=in_, scalar1=1.0, scalar2=0.0, op0=MULT, op1=ADD)
+
+        def load_q(b, k):
+            qraw[b] = slot([P, 4, NQ], f"qraw{b}", k)
+            nc.sync.dma_start(out=qraw[b][:], in_=qT[b].rearrange("(p t) q -> p t q", t=4))
+
+        def load_ch():
+            tile["ch"] = slot([P, D], "ch_sb", 3)
+            nc.sync.dma_start(out=tile["ch"][:], in_=ch)
+
+        def load_ts(k):
+            tile["ts"] = slot([P, T], "tsw", k)
+            nc.sync.dma_start(out=tile["ts"][:], in_=ts)
+
+        def ts_gather(b):
+            nc.vector.tensor_copy(tsg[:, b * N:(b + 1) * N], tile["ts"][:].indirect(offsets[:, b * 32:(b + 1) * 32]))
+
+        def ts4_turn(b):
+            tile["t4", b] = bank("tps")
+            for s in range(4):
+                nc.tensor.transpose(tile["t4", b][:, s * P:(s + 1) * P], tsg[:, b * N + s:(b + 1) * N:4], ident[:])
+
+        def ts4_out(b):
+            nc.scalar.copy(out=ts4[b][:], in_=tile["t4", b][:, 0:512:P])
+
+        def gather(t):
+            nc.vector.tensor_copy(g[:, t, :], planes[t][:].indirect(offsets[:]))
+
+        def gather3(b, h):
+            k = 2 * b + h
+            nc.vector.tensor_copy(g[:, 3, k * H:(k + 1) * H], planes[3][:].indirect(offsets[:, k * 16:(k + 1) * 16]))
+
+        def cast(t, eng):
+            copy(eng, vb[t][:], g[:, t, :])
+
+        def turn(t):
+            words = vb[t][:].bitcast(F32)
+            tile["v", t] = bank("vps")
             for b in range(B):
                 for u in range(2):
                     k = 2 * b + u
-                    nc.tensor.transpose(vps[:, k * P:(k + 1) * P], words[:, b * N // 2 + u:(b + 1) * N // 2:2], ident[:])
-            for b in range(B):
-                nc.scalar.copy(out=vtw[b][:, t * P:(t + 1) * P, :],
-                               in_=vps[:, b * 2 * P:(b + 1) * 2 * P].rearrange("m (u d) -> m d u", u=2))
+                    nc.tensor.transpose(tile["v", t][:, k * P:(k + 1) * P], words[:, b * H + u:(b + 1) * H:2], ident[:])
 
-        def quant_values(u, b):
-            cols = slice(u * 2 * P, (u + 1) * 2 * P)
-            nc.vector.quantize_mx(
-                out=vq[b][:, cols].bitcast(FP8X4), scales=vs[b][:, cols],
-                in_=vt[b][:, cols, :].rearrange("m d s -> m (d s)"))
+        def values(t, b):
+            nc.scalar.copy(out=vtw[b][:, :, t, :, :],
+                           in_=tile["v", t][:, b * 2 * P:(b + 1) * 2 * P].rearrange("m (u h p) -> m h p u", u=2, h=2))
 
-        qi = sb([P, B, NQ, 4], BF16, "qi")
-        qq = sb([P, B * NQ], U32, "qq")
-        qs = sb([P, B * NQ], U8, "qs")
+        def quant_values(h, b):
+            cols = slice(h * H, (h + 1) * H)
+            nc.vector.quantize_mx(out=vq[b][:, cols].bitcast(FP8X4), scales=vs[b][:, cols],
+                                  in_=vt[b][:, h].rearrange("m t p s -> m (t p s)"))
 
-        def queries(b):
-            qc = slice(b * NQ, (b + 1) * NQ)
-            nc.scalar.copy(out=qi[:, b], in_=qraw[:, b].rearrange("p t q -> p q t"))
-            nc.vector.quantize_mx(out=qq[:, qc].bitcast(FP8X4), scales=qs[:, qc], in_=qi[:, b].rearrange("p q t -> p (q t)"))
+        def query(b, eng):
+            copy(eng, qi[b][:], qraw[b][:].rearrange("p t q -> p q t"))
 
-        ki = [[sb([P, N // 2, 4], BF16, f"ki{b}_{h}") for h in range(2)] for b in range(B)]
-        kq = [sb([P, N], U32, f"kq{b}") for b in range(B)]
-        ks = [sb([P, N], U8, f"ks{b}") for b in range(B)]
-        sps = [psum.tile([P, N], F32, name=f"sps{b}") for b in range(B)]
+        def quant_query(b):
+            nc.vector.quantize_mx(out=qq[b][:].bitcast(FP8X4), scales=qs[b][:], in_=qi[b][:].rearrange("p q t -> p (q t)"))
 
         def keys(b, h, eng):
-            lo = b * N + h * N // 2
-            x = g[:, :, lo:lo + N // 2].rearrange("p t s -> p s t")
-            if eng == "A":
-                nc.scalar.copy(out=ki[b][h][:], in_=x)
-            else:
-                nc.vector.tensor_copy(out=ki[b][h][:], in_=x)
+            lo = b * N + h * H
+            copy(eng, ki[b][h][:], g[:, :, lo:lo + H].rearrange("p t s -> p s t"))
 
-        def scores(b, h):
-            hc = slice(h * N // 2, (h + 1) * N // 2)
+        def quant_keys(b, h):
+            hc = slice(h * H, (h + 1) * H)
             nc.vector.quantize_mx(out=kq[b][:, hc].bitcast(FP8X4), scales=ks[b][:, hc],
                                   in_=ki[b][h][:].rearrange("p s t -> p (s t)"))
-            qc = slice(b * NQ, (b + 1) * NQ)
-            nc.tensor.matmul_mx(sps[b][:, hc], lhsT=qq[:, qc].bitcast(FP8X4), lhsT_scale=qs[:, qc],
+
+        def scores(b, h):
+            hc = slice(h * H, (h + 1) * H)
+            tile["s", b, h] = half_bank(f"sps{b}{h}", b, h)
+            nc.tensor.matmul_mx(tile["s", b, h][:, 0:H], lhsT=qq[b][:].bitcast(FP8X4), lhsT_scale=qs[b][:],
                                 rhs=kq[b][:, hc].bitcast(FP8X4), rhs_scale=ks[b][:, hc], start=True, stop=True)
 
-        def softmax(b):
-            nc.vector.scalar_tensor_tensor(out=na[b][:, 0:N], in0=sps[b][:], scalar=-1.0, in1=tsg[:, slots(b)], op0=MULT, op1=MULT)
+        def scaled(b, h):
+            hc = slice(h * H, (h + 1) * H)
+            nc.vector.scalar_tensor_tensor(out=na[b][:, hc], in0=tile["s", b, h][:, 0:H], scalar=-1.0,
+                                           in1=tsg[:, b * N + h * H:b * N + (h + 1) * H], op0=MULT, op1=MULT)
+
+        def row_min(b):
             nc.vector.tensor_reduce(out=nm[b][:], in_=na[b][:, 0:N + 1], axis=AX, op=MIN)
-            p = sb([P, 4, 129], F32, f"p{b}")
-            nc.scalar.activation(out=p[:].rearrange("q s m -> q m s"), in_=na[b][:].rearrange("q (m s) -> q m s", s=4),
-                                 func=EXP, bias=nm[b][:], scale=-1.0, accum_out=l[b][:])
-            pps = bank("pps", (P, 4, P))
-            for s in range(4):
-                nc.tensor.transpose(pps[:, s, :], p[:, s, 0:P], ident[:])
-            wi = sb([P, NQ, 4], BF16, f"wi{b}")
-            nc.vector.tensor_tensor(out=wi[:], in0=pps[:].rearrange("m s q -> m q s"),
+
+        def expo(b, i):
+            nc.scalar.activation(out=p[b][:, 2 * i:2 * i + 2, :].rearrange("q s m -> q m s"),
+                                 in_=na[b][:].rearrange("q (m s) -> q m s", s=4)[:, :, 2 * i:2 * i + 2],
+                                 func=EXP, bias=nm[b][:], scale=-1.0, accum_out=l2[b][:, i:i + 1])
+
+        def turn_p(b, i):
+            if ("p", b) not in tile:
+                tile["p", b] = bank("pps")
+            for s in (2 * i, 2 * i + 1):
+                nc.tensor.transpose(tile["p", b][:, s * P:(s + 1) * P], p[b][:, s, 0:P], ident[:])
+
+        def weights(b):
+            nc.vector.tensor_tensor(out=wi[b][:], in0=tile["p", b][:].rearrange("m (s q) -> m q s", s=4),
                                     in1=ts4[b][:].unsqueeze(1).to_broadcast([P, NQ, 4]), op=MULT)
-            wq = sb([P, NQ], U32, f"wq{b}")
-            ws = sb([P, NQ], U8, f"ws{b}")
-            nc.vector.quantize_mx(out=wq[:].bitcast(FP8X4), scales=ws[:], in_=wi[:].rearrange("m q s -> m (q s)"))
-            return wq, ws
 
-        def finish(b, wq, ws):
-            nc.vector.reciprocal(out=rl[b][:], in_=l[b][:])
-            yps = psum.tile([P, D], F32, name=f"yps{b}")
-            nc.tensor.matmul_mx(yps[:], lhsT=wq[:].bitcast(FP8X4), lhsT_scale=ws[:],
-                                rhs=vq[b][:].bitcast(FP8X4), rhs_scale=vs[b][:], start=True, stop=True)
-            o = sb([P, D], F32, f"o{b}")
+        def quant_weights(b):
+            nc.vector.quantize_mx(out=wq[b][:].bitcast(FP8X4), scales=ws[b][:], in_=wi[b][:].rearrange("m q s -> m (q s)"))
+
+        def recip(b):
+            nc.vector.tensor_tensor(out=rl[b][:], in0=l2[b][:, 0:1], in1=l2[b][:, 1:2], op=ADD)
+            nc.vector.reciprocal(out=rl[b][:], in_=rl[b][:])
+
+        def product(b, h):
+            cols = slice(h * H, (h + 1) * H)
+            tile["y", b, h] = half_bank(f"yps{b}{h}", b, h)
+            nc.tensor.matmul_mx(tile["y", b, h][:, 0:H], lhsT=wq[b][:].bitcast(FP8X4), lhsT_scale=ws[b][:],
+                                rhs=vq[b][:, cols].bitcast(FP8X4), rhs_scale=vs[b][:, cols], start=True, stop=True)
+
+        def epilogue(b, h):
+            cols = slice(h * H, (h + 1) * H)
             nc.vector.scalar_tensor_tensor(
-                out=o[:].rearrange("q (p t) -> q p t", t=4), in0=yps[:].rearrange("q (t p) -> q p t", t=4),
-                scalar=rl[b][:], in1=ch_sb[:].rearrange("q (p t) -> q p t", t=4), op0=MULT, op1=MULT)
-            nc.sync.dma_start(out=out[b], in_=o[:])
+                out=o[b][:, cols].rearrange("q (p t) -> q p t", t=4), in0=tile["y", b, h][:, 0:H].rearrange("q (t p) -> q p t", t=4),
+                scalar=rl[b][:], in1=tile["ch"][:, cols].rearrange("q (p t) -> q p t", t=4), op0=MULT, op1=MULT)
 
-        scales_road()
+        def store(b, h):
+            cols = slice(h * H, (h + 1) * H)
+            nc.sync.dma_start(out=out[b][:, cols], in_=o[b][:, cols])
+
         gather(0)
-        qraw = keep.tile([P, B, 4, NQ], F32, name="qraw", tag="r0", bufs=1, align_bytes=64)
-        for b in range(B):
-            nc.sync.dma_start(out=qraw[:, b], in_=qT[b].rearrange("(p t) q -> p t q", t=4))
-        ch_sb = sb([P, D], F32, "ch_sb")
-        nc.sync.dma_start(out=ch_sb[:], in_=ch)
-        values(0, "D")
         gather(1)
-        values(1, "D")
-        scales_gather()
         gather(2)
-        values(2, "D")
-        gather(3, 0)
-        keys(0, 0, "D")
-        queries(0)
+        gather3(0, 0)
+        load_q(0, 0)
+        cast(1, "A")
+        load_q(1, 1)
+        gather3(0, 1)
+        query(0, "D")
+        cast(0, "A")
+        turn(0)
+        keys(0, 0, "A")
+        gather3(1, 0)
+        load_ts(2)
+        query(1, "D")
         keys(0, 1, "A")
-        scores(0, 0)
+        gather3(1, 1)
+        quant_keys(0, 0)
+        quant_query(0)
+        cast(2, "A")
+        keys(1, 1, "D")
+        keys(1, 0, "A")
+        quant_keys(0, 1)
+        ts_gather(0)
+        quant_keys(1, 1)
         scores(0, 1)
-        quant_values(0, 0)
-        quant_values(0, 1)
-        w0 = softmax(0)
-        gather(3, 1)
-        keys(1, 0, "D")
-        queries(1)
-        keys(1, 1, "A")
+        quant_keys(1, 0)
+        quant_query(1)
+        scores(0, 0)
+        turn(1)
+        scaled(0, 1)
+        load_ch()
         scores(1, 0)
+        turn(2)
+        ts4_turn(0)
         scores(1, 1)
-        w1 = softmax(1)
-        values(3, "A")
+        scaled(0, 0)
+        ts_gather(1)
+        values(0, 0)
+        scaled(1, 0)
+        scaled(1, 1)
+        row_min(0)
+        expo(0, 0)
+        cast(3, "A")
+        values(2, 0)
+        row_min(1)
+        values(1, 1)
+        turn(3)
+        values(1, 0)
+        ts4_turn(1)
+        values(3, 0)
         quant_values(1, 0)
-        finish(0, w0[0], w0[1])
+        expo(1, 1)
+        ts4_out(0)
+        quant_values(0, 0)
+        turn_p(0, 0)
+        values(0, 1)
+        values(2, 1)
+        turn_p(1, 1)
+        expo(0, 1)
+        values(3, 1)
+        expo(1, 0)
+        ts4_out(1)
+        turn_p(0, 1)
+        recip(1)
+        quant_values(0, 1)
+        weights(0)
+        quant_weights(0)
+        turn_p(1, 0)
         quant_values(1, 1)
-        finish(1, w1[0], w1[1])
+        weights(1)
+        quant_weights(1)
+        product(1, 0)
+        product(0, 0)
+        product(1, 1)
+        epilogue(1, 1)
+        epilogue(1, 0)
+        store(1, 1)
+        product(0, 1)
+        store(1, 0)
+        recip(0)
+        epilogue(0, 0)
+        store(0, 0)
+        epilogue(0, 1)
+        store(0, 1)

from contextlib import ExitStack

import concourse.mybir as mybir
from concourse.masks import make_identity

B, N, T, D, NQ = 2, 512, 2048, 512, 128
P = 128
H = N // 2
FLOPS = 4 * B * N * D * NQ

F32 = mybir.dt.float32
BF16 = mybir.dt.bfloat16
U32 = mybir.dt.uint32
U16 = mybir.dt.uint16
U8 = mybir.dt.uint8
FP8X4 = mybir.dt.float8_e4m3fn_x4
MULT = mybir.AluOpType.mult
ADD = mybir.AluOpType.add
MIN = mybir.AluOpType.min
EXP = mybir.ActivationFunctionType.Exp
AX = mybir.AxisListType.X


def tile_attend_x_mla_sink_kernel(tc, qT, cT, ts, sink, ch, offs, out):
    nc = tc.nc
    with ExitStack() as ctx:
        lists = ctx.enter_context(tc.tile_pool(name="lists", bufs=1))
        keep = ctx.enter_context(tc.tile_pool(name="keep", bufs=1))
        psum = ctx.enter_context(tc.psum_pool(name="psum", bufs=1))

        def sb(shape, dtype, name):
            return keep.tile(shape, dtype, name=name, align_bytes=64)

        def slot(shape, name, k):
            return keep.tile(shape, F32, name=name, tag=f"r{k}", bufs=1, align_bytes=64)

        def bank(name):
            return psum.tile([P, 512], F32, name=name, tag="x", bufs=4)

        def half_bank(name, b, h):
            return psum.tile([P, 512], F32, name=name, tag=f"s{b}{h}", bufs=1)

        offsets = lists.tile([P, B * N // 16], U16, name="offsets")
        nc.sync.dma_start(offsets[:], offs)
        ident = sb([P, P], F32, "ident")
        make_identity(nc, ident[:])
        sink_sb = sb([P, B], F32, "sink_sb")
        nc.scalar.dma_start(out=sink_sb[:], in_=sink.rearrange("b q o -> q (b o)"))

        cv = cT.rearrange("(p t) c -> p t c", t=4)
        planes = []
        for t in range(4):
            pl = slot([P, T], f"plane{t}", t)
            nc.sync.dma_start(out=pl[:], in_=cv[:, t, :])
            planes.append(pl)

        warm = sb([P, 1], F32, "warm")
        nc.gpsimd.memset(warm[:], 0.0)
        nc.scalar.activation(out=warm[:], in_=warm[:], func=EXP)

        na = [sb([P, 516], F32, f"na{b}") for b in range(B)]
        for b in range(B):
            nc.gpsimd.memset(na[b][:, 512:516], 2.0 ** 126)
            nc.gpsimd.tensor_scalar(out=na[b][:, 512:513], in0=sink_sb[:, b:b + 1], scalar1=-1.0, scalar2=0.0, op0=MULT, op1=ADD)
        nm = [sb([P, 1], F32, f"nm{b}") for b in range(B)]
        l2 = [sb([P, 2], F32, f"l2_{b}") for b in range(B)]
        rl = [sb([P, 1], F32, f"rl{b}") for b in range(B)]
        g = sb([P, 4, B * N], F32, "g")
        vb = [sb([P, B * N], BF16, f"vb{t}") for t in range(4)]
        vt = [sb([P, 2, 4, 64, 4], BF16, f"vt{b}") for b in range(B)]
        vtw = [v[:].rearrange("m h t p s -> m (h t p s)").bitcast(F32).rearrange("m (h t p u) -> m h t p u", h=2, t=4, u=2) for v in vt]
        vq = [sb([P, D], U32, f"vq{b}") for b in range(B)]
        vs = [sb([P, D], U8, f"vs{b}") for b in range(B)]
        tsg = sb([P, B * N], F32, "tsg")
        ts4 = [sb([P, 4], F32, f"ts4_{b}") for b in range(B)]
        qi = [sb([P, NQ, 4], BF16, f"qi{b}") for b in range(B)]
        qq = [sb([P, NQ], U32, f"qq{b}") for b in range(B)]
        qs = [sb([P, NQ], U8, f"qs{b}") for b in range(B)]
        ki = [[sb([P, H, 4], BF16, f"ki{b}_{h}") for h in range(2)] for b in range(B)]
        kq = [sb([P, N], U32, f"kq{b}") for b in range(B)]
        ks = [sb([P, N], U8, f"ks{b}") for b in range(B)]
        p = [sb([P, 4, 129], F32, f"p{b}") for b in range(B)]
        wi = [sb([P, NQ, 4], BF16, f"wi{b}") for b in range(B)]
        wq = [sb([P, NQ], U32, f"wq{b}") for b in range(B)]
        ws = [sb([P, NQ], U8, f"ws{b}") for b in range(B)]
        o = [sb([P, D], F32, f"o{b}") for b in range(B)]
        qraw = [None, None]
        tile = {}

        def copy(eng, out, in_):
            if eng == "A":
                nc.scalar.copy(out=out, in_=in_)
            elif eng == "D":
                nc.vector.tensor_copy(out=out, in_=in_)
            else:
                nc.gpsimd.tensor_scalar(out=out, in0=in_, scalar1=1.0, scalar2=0.0, op0=MULT, op1=ADD)

        def load_q(b, k):
            qraw[b] = slot([P, 4, NQ], f"qraw{b}", k)
            nc.sync.dma_start(out=qraw[b][:], in_=qT[b].rearrange("(p t) q -> p t q", t=4))

        def load_ch():
            tile["ch"] = slot([P, D], "ch_sb", 3)
            nc.sync.dma_start(out=tile["ch"][:], in_=ch)

        def load_ts(k):
            tile["ts"] = slot([P, T], "tsw", k)
            nc.sync.dma_start(out=tile["ts"][:], in_=ts)

        def ts_gather(b):
            nc.vector.tensor_copy(tsg[:, b * N:(b + 1) * N], tile["ts"][:].indirect(offsets[:, b * 32:(b + 1) * 32]))

        def ts4_turn(b):
            tile["t4", b] = bank("tps")
            for s in range(4):
                nc.tensor.transpose(tile["t4", b][:, s * P:(s + 1) * P], tsg[:, b * N + s:(b + 1) * N:4], ident[:])

        def ts4_out(b):
            nc.scalar.copy(out=ts4[b][:], in_=tile["t4", b][:, 0:512:P])

        def gather(t):
            nc.vector.tensor_copy(g[:, t, :], planes[t][:].indirect(offsets[:]))

        def gather3(b, h):
            k = 2 * b + h
            nc.vector.tensor_copy(g[:, 3, k * H:(k + 1) * H], planes[3][:].indirect(offsets[:, k * 16:(k + 1) * 16]))

        def cast(t, eng):
            copy(eng, vb[t][:], g[:, t, :])

        def turn(t):
            words = vb[t][:].bitcast(F32)
            tile["v", t] = bank("vps")
            for b in range(B):
                for u in range(2):
                    k = 2 * b + u
                    nc.tensor.transpose(tile["v", t][:, k * P:(k + 1) * P], words[:, b * H + u:(b + 1) * H:2], ident[:])

        def values(t, b):
            nc.scalar.copy(out=vtw[b][:, :, t, :, :],
                           in_=tile["v", t][:, b * 2 * P:(b + 1) * 2 * P].rearrange("m (u h p) -> m h p u", u=2, h=2))

        def quant_values(h, b):
            cols = slice(h * H, (h + 1) * H)
            nc.vector.quantize_mx(out=vq[b][:, cols].bitcast(FP8X4), scales=vs[b][:, cols],
                                  in_=vt[b][:, h].rearrange("m t p s -> m (t p s)"))

        def query(b, eng):
            copy(eng, qi[b][:], qraw[b][:].rearrange("p t q -> p q t"))

        def quant_query(b):
            nc.vector.quantize_mx(out=qq[b][:].bitcast(FP8X4), scales=qs[b][:], in_=qi[b][:].rearrange("p q t -> p (q t)"))

        def keys(b, h, eng):
            lo = b * N + h * H
            copy(eng, ki[b][h][:], g[:, :, lo:lo + H].rearrange("p t s -> p s t"))

        def quant_keys(b, h):
            hc = slice(h * H, (h + 1) * H)
            nc.vector.quantize_mx(out=kq[b][:, hc].bitcast(FP8X4), scales=ks[b][:, hc],
                                  in_=ki[b][h][:].rearrange("p s t -> p (s t)"))

        def scores(b, h):
            hc = slice(h * H, (h + 1) * H)
            tile["s", b, h] = half_bank(f"sps{b}{h}", b, h)
            nc.tensor.matmul_mx(tile["s", b, h][:, 0:H], lhsT=qq[b][:].bitcast(FP8X4), lhsT_scale=qs[b][:],
                                rhs=kq[b][:, hc].bitcast(FP8X4), rhs_scale=ks[b][:, hc], start=True, stop=True)

        def scaled(b, h):
            hc = slice(h * H, (h + 1) * H)
            nc.vector.scalar_tensor_tensor(out=na[b][:, hc], in0=tile["s", b, h][:, 0:H], scalar=-1.0,
                                           in1=tsg[:, b * N + h * H:b * N + (h + 1) * H], op0=MULT, op1=MULT)

        def row_min(b):
            nc.vector.tensor_reduce(out=nm[b][:], in_=na[b][:, 0:N + 1], axis=AX, op=MIN)

        def expo(b, i):
            nc.scalar.activation(out=p[b][:, 2 * i:2 * i + 2, :].rearrange("q s m -> q m s"),
                                 in_=na[b][:].rearrange("q (m s) -> q m s", s=4)[:, :, 2 * i:2 * i + 2],
                                 func=EXP, bias=nm[b][:], scale=-1.0, accum_out=l2[b][:, i:i + 1])

        def turn_p(b, i):
            if ("p", b) not in tile:
                tile["p", b] = bank("pps")
            for s in (2 * i, 2 * i + 1):
                nc.tensor.transpose(tile["p", b][:, s * P:(s + 1) * P], p[b][:, s, 0:P], ident[:])

        def weights(b):
            nc.vector.tensor_tensor(out=wi[b][:], in0=tile["p", b][:].rearrange("m (s q) -> m q s", s=4),
                                    in1=ts4[b][:].unsqueeze(1).to_broadcast([P, NQ, 4]), op=MULT)

        def quant_weights(b):
            nc.vector.quantize_mx(out=wq[b][:].bitcast(FP8X4), scales=ws[b][:], in_=wi[b][:].rearrange("m q s -> m (q s)"))

        def recip(b):
            nc.vector.tensor_tensor(out=rl[b][:], in0=l2[b][:, 0:1], in1=l2[b][:, 1:2], op=ADD)
            nc.vector.reciprocal(out=rl[b][:], in_=rl[b][:])

        def product(b, h):
            cols = slice(h * H, (h + 1) * H)
            tile["y", b, h] = half_bank(f"yps{b}{h}", b, h)
            nc.tensor.matmul_mx(tile["y", b, h][:, 0:H], lhsT=wq[b][:].bitcast(FP8X4), lhsT_scale=ws[b][:],
                                rhs=vq[b][:, cols].bitcast(FP8X4), rhs_scale=vs[b][:, cols], start=True, stop=True)

        def epilogue(b, h):
            cols = slice(h * H, (h + 1) * H)
            nc.vector.scalar_tensor_tensor(
                out=o[b][:, cols].rearrange("q (p t) -> q p t", t=4), in0=tile["y", b, h][:, 0:H].rearrange("q (t p) -> q p t", t=4),
                scalar=rl[b][:], in1=tile["ch"][:, cols].rearrange("q (p t) -> q p t", t=4), op0=MULT, op1=MULT)

        def store(b, h):
            cols = slice(h * H, (h + 1) * H)
            nc.sync.dma_start(out=out[b][:, cols], in_=o[b][:, cols])

        gather(0)
        gather(1)
        gather(2)
        gather3(0, 0)
        load_q(0, 0)
        cast(1, "A")
        load_q(1, 1)
        gather3(0, 1)
        query(0, "D")
        cast(0, "A")
        turn(0)
        keys(0, 0, "A")
        gather3(1, 0)
        load_ts(2)
        query(1, "D")
        keys(0, 1, "A")
        gather3(1, 1)
        quant_keys(0, 0)
        quant_query(0)
        cast(2, "A")
        keys(1, 1, "D")
        keys(1, 0, "A")
        quant_keys(0, 1)
        ts_gather(0)
        quant_keys(1, 1)
        scores(0, 1)
        quant_keys(1, 0)
        quant_query(1)
        scores(0, 0)
        turn(1)
        scaled(0, 1)
        load_ch()
        scores(1, 0)
        turn(2)
        ts4_turn(0)
        scores(1, 1)
        scaled(0, 0)
        ts_gather(1)
        values(0, 0)
        scaled(1, 0)
        scaled(1, 1)
        row_min(0)
        expo(0, 0)
        cast(3, "A")
        values(2, 0)
        row_min(1)
        values(1, 1)
        turn(3)
        values(1, 0)
        ts4_turn(1)
        values(3, 0)
        quant_values(1, 0)
        expo(1, 1)
        ts4_out(0)
        quant_values(0, 0)
        turn_p(0, 0)
        values(0, 1)
        values(2, 1)
        turn_p(1, 1)
        expo(0, 1)
        values(3, 1)
        expo(1, 0)
        ts4_out(1)
        turn_p(0, 1)
        recip(1)
        quant_values(0, 1)
        weights(0)
        quant_weights(0)
        turn_p(1, 0)
        quant_values(1, 1)
        weights(1)
        quant_weights(1)
        product(1, 0)
        product(0, 0)
        product(1, 1)
        epilogue(1, 1)
        epilogue(1, 0)
        store(1, 1)
        product(0, 1)
        store(1, 0)
        recip(0)
        epilogue(0, 0)
        store(0, 0)
        epilogue(0, 1)
        store(0, 1)
